import numpy as np
import ml_dtypes


def mxq(x, axis, fmt="e4m3"):
    dtype, down = {"e4m3": (ml_dtypes.float8_e4m3fn, 7), "e5m2": (ml_dtypes.float8_e5m2, 14)}[fmt]
    v = np.moveaxis(np.asarray(x, np.float32).astype(ml_dtypes.bfloat16).astype(np.float64), axis, -1)
    blocks = v.reshape(v.shape[:-1] + (-1, 32))
    amax = np.abs(blocks).max(-1, keepdims=True)
    byte = np.maximum(np.where(amax > 0, np.frexp(amax)[1] - 1 + 127, 0) - down, 1)
    scale = np.exp2(byte - 127.0)
    codes = (blocks / scale).astype(np.float32).astype(dtype).astype(np.float64)
    return np.moveaxis((codes * scale).reshape(v.shape), -1, axis)


WIDE = False


def mx_kscale(k):
    if not WIDE:
        return np.ones(k)
    levels = np.array([10, -10, 5, -5, 0])
    if k % 512:
        return np.exp2(np.random.permutation(np.resize(levels, k // 32))).repeat(32)
    a = np.empty((k // 512, 16))
    for p in range(k // 512):
        a[p, :8] = np.random.permutation(np.resize(levels, 8))
        for g in range(8):
            far = levels[np.abs(levels - a[p, g]) >= 10]
            a[p, g + 8] = far[np.random.randint(len(far))]
    return np.exp2(a.ravel()).repeat(32)


def f64(x):
    return np.asarray(x).astype(np.float64)


def striped(idx):
    return np.tile(np.asarray(idx).reshape(-1, 16).T, (8, 1)).astype(np.uint16)


def unstriped(offs):
    return offs[:16].T.reshape(-1).astype(np.int64)


E2M1 = np.array([0.0, 0.5, 1.0, 1.5, 2.0, 3.0, 4.0, 6.0, -0.0, -0.5, -1.0, -1.5, -2.0, -3.0, -4.0, -6.0])


def pack_weight(w, fmt):
    k, n = w.shape
    w = f64(np.asarray(w, np.float32).astype(ml_dtypes.bfloat16)).reshape(k // 32, 32, n)
    amax = np.abs(w).max(1)
    if fmt == "e4m3":
        byte = np.frexp(amax)[1] - 1 + 127 - 7
    else:
        mant, ex = np.frexp(amax / 6.0)
        byte = np.where(mant > 0.5, ex, ex - 1) + 127
    byte = np.clip(np.where(amax > 0, byte, 1), 1, 254)
    scaled = (w * np.exp2(127.0 - byte)[:, None, :]).reshape(k, n).astype(np.float32)
    by_word = np.ascontiguousarray(scaled.reshape(k // 512, 128, 4, n).transpose(0, 1, 3, 2))
    if fmt == "e4m3":
        words = by_word.astype(ml_dtypes.float8_e4m3fn).view(np.uint8)
    else:
        c = by_word.astype(ml_dtypes.float4_e2m1fn).view(np.uint8) & 0xF
        words = (c[..., 0::2] | (c[..., 1::2] << 4)).reshape(k // 512, 128, 2 * n)
    return np.ascontiguousarray(words), np.ascontiguousarray(byte.astype(np.uint8).reshape(k // 512, 16, n))


def unpack_weight(words, scales, fmt):
    g, _, n = scales.shape
    words = np.ascontiguousarray(words).reshape(g, 128, n, -1)
    if fmt == "e4m3":
        vals = words.view(ml_dtypes.float8_e4m3fn).astype(np.float64)
    else:
        nib = np.empty((g, 128, n, 4), np.uint8)
        nib[..., 0::2] = words & 0xF
        nib[..., 1::2] = words >> 4
        vals = E2M1[nib]
    vals = vals * np.repeat(np.exp2(scales.astype(np.float64) - 127.0), 8, axis=1)[..., None]
    return vals.transpose(0, 1, 3, 2).reshape(g * 512, n)


B, N, T, D, NQ = 1, 1024, 4096, 512, 128
SEG = 32


def setup_inputs():
    n = np.random.standard_normal
    pages = np.random.permutation(T // 32)[:B * N // 32]
    idx = (pages[:, None] * 32 + np.arange(32)[None, :]).reshape(-1)
    s = mx_kscale(D)[:, None]
    kp = pack_weight(n((D, T)) / s, "e4m3")
    return {
        "qT": (n((B, D, NQ)) * s * (1.00 / np.sqrt(D))).astype(np.float32),
        "k_words": kp[0],
        "k_scales": kp[1],
        "offs": striped(idx),
    }


def reference(qT, k_words, k_scales, offs):
    idx = unstriped(offs)
    pick = lambda x, which: x[:, which].reshape(x.shape[0], B, -1).transpose(1, 0, 2)
    k = unpack_weight(k_words, k_scales, "e4m3")
    kg = pick(k, idx)
    qq = mxq(f64(qT), 1, "e4m3")
    a = qq.transpose(0, 2, 1) @ kg
    y = np.log(np.exp(2.0 * a).reshape(B, NQ, N // SEG, SEG).sum(-1))
    return y

@@ -1,0 +1,137 @@
+from contextlib import ExitStack
+
+import concourse.mybir as mybir
+
+F32 = mybir.dt.float32
+BF16 = mybir.dt.bfloat16
+I32 = mybir.dt.int32
+U32 = mybir.dt.uint32
+U16 = mybir.dt.uint16
+U8 = mybir.dt.uint8
+FP8X4 = mybir.dt.float8_e4m3fn_x4
+ALU = mybir.AluOpType
+ACT = mybir.ActivationFunctionType
+AXIS_X = mybir.AxisListType.X
+
+P = 128
+PACK = 4
+D, T, N, NQ, SEG = 512, 4096, 1024, 128, 32
+PAGES = N // SEG
+HALF = 512
+CHUNK = 128
+CHUNK_PAGES = CHUNK // SEG
+WIDE = (4, 5, 6, 7)
+WORD_LOADS = 2
+
+FLOPS = 2 * NQ * N * D
+BYTES = D * NQ * 4 + T * P * 4 + 16 * T + P * 64 * 2 + NQ * PAGES * 4
+
+
+def tile_attend_pagelse_kernel(tc, qT, k_words, k_scales, offs, out):
+    nc = tc.nc
+
+    with ExitStack() as ctx:
+        sb = ctx.enter_context(tc.tile_pool(name="sb", bufs=1))
+        ps = ctx.enter_context(tc.psum_pool(name="ps", bufs=1))
+
+        offsets = sb.tile([P, N // 16], U16, name="offsets")
+        pool_words = sb.tile([P, T], I32, name="pool_words", align_bytes=64)
+        pool_scales = sb.tile([P, T], U8, name="pool_scales", align_bytes=64)
+        q_raw = sb.tile([P, PACK, NQ], F32, name="q_raw", align_bytes=64)
+        q_bf = sb.tile([P, NQ, PACK], BF16, name="q_bf", align_bytes=64)
+        q_codes = sb.tile([P, NQ], U32, name="q_codes", align_bytes=64)
+        q_scales = sb.tile([P, NQ], U8, name="q_scales", align_bytes=64)
+        key_words = [sb.tile([P, HALF], U32, name="key_words%d" % h, align_bytes=64) for h in range(N // HALF)]
+        key_scales = sb.tile([P, N], U8, name="key_scales", align_bytes=64)
+
+        nc.vector.memset(pool_scales[:].bitcast(I32), 0)
+        nc.sync.dma_start(offsets[:], offs)
+        nc.sync.dma_start(out=q_raw[:], in_=qT[0].rearrange("(p t) q -> p t q", t=PACK))
+        for quad in range(4):
+            nc.scalar.dma_start(
+                out=pool_scales[32 * quad : 32 * quad + 4, :].bitcast(I32),
+                in_=k_scales[0, 4 * quad : 4 * quad + 4, :].bitcast(I32),
+            )
+        words_hbm = k_words[0].rearrange("p n t -> p (n t)").bitcast(I32)
+        step = T // WORD_LOADS
+        for c in range(WORD_LOADS):
+            nc.sync.dma_start(out=pool_words[:, c * step : (c + 1) * step], in_=words_hbm[:, c * step : (c + 1) * step])
+
+        nc.scalar.activation(out=q_bf[:], in_=q_raw[:].rearrange("p t q -> p q t"), func=ACT.Copy, scale=-2.0)
+        nc.vector.quantize_mx(out=q_codes[:].bitcast(FP8X4), scales=q_scales[:], in_=q_bf[:].rearrange("p q t -> p (q t)"))
+
+        nc.vector.tensor_copy(key_scales[:], pool_scales[:].indirect(offsets[:]))
+        cols = HALF // 16
+        for h in range(N // HALF):
+            nc.vector.tensor_copy(key_words[h][:], pool_words[:].bitcast(U32).indirect(offsets[:, h * cols : (h + 1) * cols]))
+
+        least = sb.tile([P, PAGES], F32, name="least")
+        sums = sb.tile([P, PAGES], F32, name="sums")
+        scores = []
+        for c in range(N // CHUNK):
+            bank = ps.tile([NQ, CHUNK], F32, name="bank%d" % c)
+            h, first = divmod(c * CHUNK, HALF)
+            nc.tensor.matmul_mx(
+                out=bank[:],
+                lhsT=q_codes[:].bitcast(FP8X4),
+                lhsT_scale=q_scales[:],
+                rhs=key_words[h][:, first : first + CHUNK].bitcast(FP8X4),
+                rhs_scale=key_scales[:, c * CHUNK : (c + 1) * CHUNK],
+                start=True,
+                stop=True,
+            )
+            scores.append(bank[:].rearrange("q (j i) -> q j i", i=SEG))
+
+        def pages_of(c):
+            return slice(c * CHUNK_PAGES, (c + 1) * CHUNK_PAGES)
+
+        terms = [sb.tile([P, CHUNK_PAGES, SEG], F32, name="terms%d" % c) for c in range(N // CHUNK)]
+        shifted = {c: sb.tile([P, CHUNK_PAGES, SEG], F32, name="shifted%d" % c) for c in WIDE}
+
+        def find_least(c):
+            nc.vector.tensor_reduce(out=least[:, pages_of(c)], in_=scores[c], axis=AXIS_X, op=ALU.min)
+
+        def by_page(c):
+            for j in range(CHUNK_PAGES):
+                page = c * CHUNK_PAGES + j
+                nc.scalar.activation(
+                    out=terms[c][:, j, :],
+                    in_=scores[c][:, j, :],
+                    func=ACT.Exp,
+                    bias=least[:, page : page + 1],
+                    scale=-1.0,
+                )
+
+        def shift(c):
+            nc.vector.tensor_tensor(
+                out=shifted[c][:],
+                in0=scores[c],
+                in1=least[:, pages_of(c)].unsqueeze(2).to_broadcast([P, CHUNK_PAGES, SEG]),
+                op=ALU.subtract,
+            )
+
+        def wide_exp(c):
+            nc.scalar.activation(out=terms[c][:], in_=shifted[c][:], func=ACT.Exp, scale=-1.0)
+
+        def wide_sum(c):
+            nc.vector.tensor_reduce(out=sums[:, pages_of(c)], in_=terms[c][:], axis=AXIS_X, op=ALU.add)
+
+        for c in range(4):
+            find_least(c)
+            by_page(c)
+        find_least(4)
+        for c in WIDE:
+            if c + 1 in WIDE:
+                find_least(c + 1)
+            shift(c)
+            wide_exp(c)
+        for c in range(N // CHUNK):
+            wide_sum(c)
+
+        logs = sb.tile([P, PAGES], F32, name="logs")
+        result = sb.tile([P, PAGES], F32, name="result")
+        early = CHUNK_PAGES
+        nc.scalar.activation(out=logs[:, :early], in_=sums[:, :early], func=ACT.Ln)
+        nc.scalar.activation(out=logs[:, early:], in_=sums[:, early:], func=ACT.Ln)
+        nc.vector.tensor_tensor(out=result[:], in0=logs[:], in1=least[:], op=ALU.subtract)
+        nc.sync.dma_start(out=out[0], in_=result[:])

@@ -42,16 +42,14 @@ def tile_attend_pagelse_kernel(tc, qT, k_words, k_scales, offs, out):
         q_codes = sb.tile([P, NQ], U32, name="q_codes", align_bytes=64)
         q_scales = sb.tile([P, NQ], U8, name="q_scales", align_bytes=64)
         key_words = [sb.tile([P, HALF], U32, name="key_words%d" % h, align_bytes=64) for h in range(N // HALF)]
+        picked_scales = sb.tile([P, N], U8, name="picked_scales", align_bytes=64)
         key_scales = sb.tile([P, N], U8, name="key_scales", align_bytes=64)
 
         nc.vector.memset(pool_scales[:].bitcast(I32), 0)
+        nc.vector.memset(key_scales[:].bitcast(I32), 0)
         nc.sync.dma_start(offsets[:], offs)
         nc.sync.dma_start(out=q_raw[:], in_=qT[0].rearrange("(p t) q -> p t q", t=PACK))
-        for quad in range(4):
-            nc.scalar.dma_start(
-                out=pool_scales[32 * quad : 32 * quad + 4, :].bitcast(I32),
-                in_=k_scales[0, 4 * quad : 4 * quad + 4, :].bitcast(I32),
-            )
+        nc.scalar.dma_start(out=pool_scales[0:P:8, :].bitcast(I32), in_=k_scales[0].bitcast(I32))
         words_hbm = k_words[0].rearrange("p n t -> p (n t)").bitcast(I32)
         step = T // WORD_LOADS
         for c in range(WORD_LOADS):
@@ -60,7 +58,12 @@ def tile_attend_pagelse_kernel(tc, qT, k_words, k_scales, offs, out):
         nc.scalar.activation(out=q_bf[:], in_=q_raw[:].rearrange("p t q -> p q t"), func=ACT.Copy, scale=-2.0)
         nc.vector.quantize_mx(out=q_codes[:].bitcast(FP8X4), scales=q_scales[:], in_=q_bf[:].rearrange("p q t -> p (q t)"))
 
-        nc.vector.tensor_copy(key_scales[:], pool_scales[:].indirect(offsets[:]))
+        nc.vector.tensor_copy(picked_scales[:], pool_scales[:].indirect(offsets[:]))
+        for quad in range(4):
+            nc.scalar.dma_start(
+                out=key_scales[32 * quad : 32 * quad + 4, :].bitcast(I32),
+                in_=picked_scales[32 * quad : 32 * quad + 32 : 8, :].bitcast(I32),
+            )
         cols = HALF // 16
         for h in range(N // HALF):
             nc.vector.tensor_copy(key_words[h][:], pool_words[:].bitcast(U32).indirect(offsets[:, h * cols : (h + 1) * cols]))
@@ -130,8 +133,6 @@ def tile_attend_pagelse_kernel(tc, qT, k_words, k_scales, offs, out):
 
         logs = sb.tile([P, PAGES], F32, name="logs")
         result = sb.tile([P, PAGES], F32, name="result")
-        early = CHUNK_PAGES
-        nc.scalar.activation(out=logs[:, :early], in_=sums[:, :early], func=ACT.Ln)
-        nc.scalar.activation(out=logs[:, early:], in_=sums[:, early:], func=ACT.Ln)
+        nc.scalar.activation(out=logs[:], in_=sums[:], func=ACT.Ln)
         nc.vector.tensor_tensor(out=result[:], in0=logs[:], in1=least[:], op=ALU.subtract)
         nc.sync.dma_start(out=out[0], in_=result[:])

@@ -20,8 +20,8 @@ PAGES = N // SEG
 HALF = 512
 CHUNK = 128
 CHUNK_PAGES = CHUNK // SEG
-WIDE = (4, 5, 6, 7)
-WORD_LOADS = 2
+WIDE = (5, 6, 7,)
+WORD_LOADS = 1
 
 FLOPS = 2 * NQ * N * D
 BYTES = D * NQ * 4 + T * P * 4 + 16 * T + P * 64 * 2 + NQ * PAGES * 4
@@ -42,14 +42,14 @@ def tile_attend_pagelse_kernel(tc, qT, k_words, k_scales, offs, out):
         q_codes = sb.tile([P, NQ], U32, name="q_codes", align_bytes=64)
         q_scales = sb.tile([P, NQ], U8, name="q_scales", align_bytes=64)
         key_words = [sb.tile([P, HALF], U32, name="key_words%d" % h, align_bytes=64) for h in range(N // HALF)]
-        picked_scales = sb.tile([P, N], U8, name="picked_scales", align_bytes=64)
+        picked_scales = [sb.tile([P, HALF], U8, name="picked_scales%d" % h, align_bytes=64) for h in range(N // HALF)]
         key_scales = sb.tile([P, N], U8, name="key_scales", align_bytes=64)
 
         nc.vector.memset(pool_scales[:].bitcast(I32), 0)
         nc.vector.memset(key_scales[:].bitcast(I32), 0)
         nc.sync.dma_start(offsets[:], offs)
         nc.sync.dma_start(out=q_raw[:], in_=qT[0].rearrange("(p t) q -> p t q", t=PACK))
-        nc.scalar.dma_start(out=pool_scales[0:P:8, :].bitcast(I32), in_=k_scales[0].bitcast(I32))
+        nc.scalar.dma_start(out=pool_scales[4:P:8, :].bitcast(I32), in_=k_scales[0].bitcast(I32))
         words_hbm = k_words[0].rearrange("p n t -> p (n t)").bitcast(I32)
         step = T // WORD_LOADS
         for c in range(WORD_LOADS):
@@ -58,13 +58,14 @@ def tile_attend_pagelse_kernel(tc, qT, k_words, k_scales, offs, out):
         nc.scalar.activation(out=q_bf[:], in_=q_raw[:].rearrange("p t q -> p q t"), func=ACT.Copy, scale=-2.0)
         nc.vector.quantize_mx(out=q_codes[:].bitcast(FP8X4), scales=q_scales[:], in_=q_bf[:].rearrange("p q t -> p (q t)"))
 
-        nc.vector.tensor_copy(picked_scales[:], pool_scales[:].indirect(offsets[:]))
-        for quad in range(4):
-            nc.scalar.dma_start(
-                out=key_scales[32 * quad : 32 * quad + 4, :].bitcast(I32),
-                in_=picked_scales[32 * quad : 32 * quad + 32 : 8, :].bitcast(I32),
-            )
         cols = HALF // 16
+        for h in range(N // HALF):
+            nc.vector.tensor_copy(picked_scales[h][:], pool_scales[:].indirect(offsets[:, h * cols : (h + 1) * cols]))
+            for quad in range(4):
+                nc.scalar.dma_start(
+                    out=key_scales[32 * quad : 32 * quad + 4, h * HALF : (h + 1) * HALF].bitcast(I32),
+                    in_=picked_scales[h][32 * quad + 4 : 32 * quad + 32 : 8, :].bitcast(I32),
+                )
         for h in range(N // HALF):
             nc.vector.tensor_copy(key_words[h][:], pool_words[:].bitcast(U32).indirect(offsets[:, h * cols : (h + 1) * cols]))
 
@@ -88,7 +89,8 @@ def tile_attend_pagelse_kernel(tc, qT, k_words, k_scales, offs, out):
         def pages_of(c):
             return slice(c * CHUNK_PAGES, (c + 1) * CHUNK_PAGES)
 
-        terms = [sb.tile([P, CHUNK_PAGES, SEG], F32, name="terms%d" % c) for c in range(N // CHUNK)]
+        all_terms = sb.tile([P, PAGES, SEG], F32, name="all_terms")
+        terms = [all_terms[:, pages_of(c), :] for c in range(N // CHUNK)]
         shifted = {c: sb.tile([P, CHUNK_PAGES, SEG], F32, name="shifted%d" % c) for c in WIDE}
 
         def find_least(c):
@@ -114,22 +116,28 @@ def tile_attend_pagelse_kernel(tc, qT, k_words, k_scales, offs, out):
             )
 
         def wide_exp(c):
-            nc.scalar.activation(out=terms[c][:], in_=shifted[c][:], func=ACT.Exp, scale=-1.0)
+            nc.scalar.activation(out=terms[c], in_=shifted[c][:], func=ACT.Exp, scale=-1.0)
 
-        def wide_sum(c):
-            nc.vector.tensor_reduce(out=sums[:, pages_of(c)], in_=terms[c][:], axis=AXIS_X, op=ALU.add)
-
-        for c in range(4):
-            find_least(c)
-            by_page(c)
+        find_least(0)
+        by_page(0)
+        find_least(1)
+        by_page(1)
+        find_least(2)
+        by_page(2)
+        find_least(3)
+        by_page(3)
         find_least(4)
-        for c in WIDE:
-            if c + 1 in WIDE:
-                find_least(c + 1)
-            shift(c)
-            wide_exp(c)
-        for c in range(N // CHUNK):
-            wide_sum(c)
+        by_page(4)
+        find_least(5)
+        find_least(6)
+        shift(5)
+        wide_exp(5)
+        find_least(7)
+        shift(6)
+        wide_exp(6)
+        shift(7)
+        wide_exp(7)
+        nc.vector.tensor_reduce(out=sums[:], in_=all_terms[:], axis=AXIS_X, op=ALU.add)
 
         logs = sb.tile([P, PAGES], F32, name="logs")
         result = sb.tile([P, PAGES], F32, name="result")

@@ -42,14 +42,14 @@ def tile_attend_pagelse_kernel(tc, qT, k_words, k_scales, offs, out):
         q_codes = sb.tile([P, NQ], U32, name="q_codes", align_bytes=64)
         q_scales = sb.tile([P, NQ], U8, name="q_scales", align_bytes=64)
         key_words = [sb.tile([P, HALF], U32, name="key_words%d" % h, align_bytes=64) for h in range(N // HALF)]
-        picked_scales = [sb.tile([P, HALF], U8, name="picked_scales%d" % h, align_bytes=64) for h in range(N // HALF)]
+        picked_scales = sb.tile([P, N], U8, name="picked_scales", align_bytes=64)
         key_scales = sb.tile([P, N], U8, name="key_scales", align_bytes=64)
 
         nc.vector.memset(pool_scales[:].bitcast(I32), 0)
         nc.vector.memset(key_scales[:].bitcast(I32), 0)
         nc.sync.dma_start(offsets[:], offs)
         nc.sync.dma_start(out=q_raw[:], in_=qT[0].rearrange("(p t) q -> p t q", t=PACK))
-        nc.scalar.dma_start(out=pool_scales[4:P:8, :].bitcast(I32), in_=k_scales[0].bitcast(I32))
+        nc.scalar.dma_start(out=pool_scales[32:96:4, :].bitcast(I32), in_=k_scales[0].bitcast(I32))
         words_hbm = k_words[0].rearrange("p n t -> p (n t)").bitcast(I32)
         step = T // WORD_LOADS
         for c in range(WORD_LOADS):
@@ -59,13 +59,12 @@ def tile_attend_pagelse_kernel(tc, qT, k_words, k_scales, offs, out):
         nc.vector.quantize_mx(out=q_codes[:].bitcast(FP8X4), scales=q_scales[:], in_=q_bf[:].rearrange("p q t -> p (q t)"))
 
         cols = HALF // 16
-        for h in range(N // HALF):
-            nc.vector.tensor_copy(picked_scales[h][:], pool_scales[:].indirect(offsets[:, h * cols : (h + 1) * cols]))
-            for quad in range(4):
-                nc.scalar.dma_start(
-                    out=key_scales[32 * quad : 32 * quad + 4, h * HALF : (h + 1) * HALF].bitcast(I32),
-                    in_=picked_scales[h][32 * quad + 4 : 32 * quad + 32 : 8, :].bitcast(I32),
-                )
+        nc.vector.tensor_copy(picked_scales[:], pool_scales[:].indirect(offsets[:]))
+        for quad in range(4):
+            nc.scalar.dma_start(
+                out=key_scales[32 * quad : 32 * quad + 4, :].bitcast(I32),
+                in_=picked_scales[32 + 16 * quad : 48 + 16 * quad : 4, :].bitcast(I32),
+            )
         for h in range(N // HALF):
             nc.vector.tensor_copy(key_words[h][:], pool_words[:].bitcast(U32).indirect(offsets[:, h * cols : (h + 1) * cols]))
 

@@ -45,11 +45,11 @@ def tile_attend_pagelse_kernel(tc, qT, k_words, k_scales, offs, out):
         picked_scales = sb.tile([P, N], U8, name="picked_scales", align_bytes=64)
         key_scales = sb.tile([P, N], U8, name="key_scales", align_bytes=64)
 
-        nc.vector.memset(pool_scales[:].bitcast(I32), 0)
+        nc.vector.memset(pool_scales[0:112, :].bitcast(I32), 0)
         nc.vector.memset(key_scales[:].bitcast(I32), 0)
         nc.sync.dma_start(offsets[:], offs)
+        nc.sync.dma_start(out=pool_scales[112:P, :].bitcast(I32), in_=k_scales[0].bitcast(I32))
         nc.sync.dma_start(out=q_raw[:], in_=qT[0].rearrange("(p t) q -> p t q", t=PACK))
-        nc.scalar.dma_start(out=pool_scales[32:96:4, :].bitcast(I32), in_=k_scales[0].bitcast(I32))
         words_hbm = k_words[0].rearrange("p n t -> p (n t)").bitcast(I32)
         step = T // WORD_LOADS
         for c in range(WORD_LOADS):
@@ -63,7 +63,7 @@ def tile_attend_pagelse_kernel(tc, qT, k_words, k_scales, offs, out):
         for quad in range(4):
             nc.scalar.dma_start(
                 out=key_scales[32 * quad : 32 * quad + 4, :].bitcast(I32),
-                in_=picked_scales[32 + 16 * quad : 48 + 16 * quad : 4, :].bitcast(I32),
+                in_=picked_scales[112 + 4 * quad : 116 + 4 * quad, :].bitcast(I32),
             )
         for h in range(N // HALF):
             nc.vector.tensor_copy(key_words[h][:], pool_words[:].bitcast(U32).indirect(offsets[:, h * cols : (h + 1) * cols]))

@@ -21,7 +21,8 @@ HALF = 512
 CHUNK = 128
 CHUNK_PAGES = CHUNK // SEG
 WIDE = (5, 6, 7,)
-WORD_LOADS = 1
+EARLY_LOADS = 2
+EARLY = 512
 
 FLOPS = 2 * NQ * N * D
 BYTES = D * NQ * 4 + T * P * 4 + 16 * T + P * 64 * 2 + NQ * PAGES * 4
@@ -45,26 +46,26 @@ def tile_attend_pagelse_kernel(tc, qT, k_words, k_scales, offs, out):
         picked_scales = sb.tile([P, N], U8, name="picked_scales", align_bytes=64)
         key_scales = sb.tile([P, N], U8, name="key_scales", align_bytes=64)
 
-        nc.vector.memset(pool_scales[0:112, :].bitcast(I32), 0)
+        nc.vector.memset(pool_scales[:].bitcast(I32), 0)
         nc.vector.memset(key_scales[:].bitcast(I32), 0)
-        nc.sync.dma_start(offsets[:], offs)
-        nc.sync.dma_start(out=pool_scales[112:P, :].bitcast(I32), in_=k_scales[0].bitcast(I32))
         nc.sync.dma_start(out=q_raw[:], in_=qT[0].rearrange("(p t) q -> p t q", t=PACK))
+        nc.sync.dma_start(offsets[:], offs)
+        nc.sync.dma_start(out=pool_scales[32:96:4, :].bitcast(I32), in_=k_scales[0].bitcast(I32))
         words_hbm = k_words[0].rearrange("p n t -> p (n t)").bitcast(I32)
-        step = T // WORD_LOADS
-        for c in range(WORD_LOADS):
-            nc.sync.dma_start(out=pool_words[:, c * step : (c + 1) * step], in_=words_hbm[:, c * step : (c + 1) * step])
+        for r in range(EARLY_LOADS):
+            nc.sync.dma_start(out=pool_words[r:P:EARLY_LOADS, 0:EARLY], in_=words_hbm[r:P:EARLY_LOADS, 0:EARLY])
+        nc.sync.dma_start(out=pool_words[:, EARLY:T], in_=words_hbm[:, EARLY:T])
 
         nc.scalar.activation(out=q_bf[:], in_=q_raw[:].rearrange("p t q -> p q t"), func=ACT.Copy, scale=-2.0)
-        nc.vector.quantize_mx(out=q_codes[:].bitcast(FP8X4), scales=q_scales[:], in_=q_bf[:].rearrange("p q t -> p (q t)"))
 
         cols = HALF // 16
         nc.vector.tensor_copy(picked_scales[:], pool_scales[:].indirect(offsets[:]))
         for quad in range(4):
             nc.scalar.dma_start(
                 out=key_scales[32 * quad : 32 * quad + 4, :].bitcast(I32),
-                in_=picked_scales[112 + 4 * quad : 116 + 4 * quad, :].bitcast(I32),
+                in_=picked_scales[32 + 16 * quad : 48 + 16 * quad : 4, :].bitcast(I32),
             )
+        nc.vector.quantize_mx(out=q_codes[:].bitcast(FP8X4), scales=q_scales[:], in_=q_bf[:].rearrange("p q t -> p (q t)"))
         for h in range(N // HALF):
             nc.vector.tensor_copy(key_words[h][:], pool_words[:].bitcast(U32).indirect(offsets[:, h * cols : (h + 1) * cols]))
 

@@ -22,7 +22,7 @@ CHUNK = 128
 CHUNK_PAGES = CHUNK // SEG
 WIDE = (5, 6, 7,)
 EARLY_LOADS = 2
-EARLY = 512
+EARLY = 1024
 
 FLOPS = 2 * NQ * N * D
 BYTES = D * NQ * 4 + T * P * 4 + 16 * T + P * 64 * 2 + NQ * PAGES * 4

@@ -43,11 +43,12 @@ def tile_attend_pagelse_kernel(tc, qT, k_words, k_scales, offs, out):
         q_codes = sb.tile([P, NQ], U32, name="q_codes", align_bytes=64)
         q_scales = sb.tile([P, NQ], U8, name="q_scales", align_bytes=64)
         key_words = [sb.tile([P, HALF], U32, name="key_words%d" % h, align_bytes=64) for h in range(N // HALF)]
-        picked_scales = sb.tile([P, N], U8, name="picked_scales", align_bytes=64)
-        key_scales = sb.tile([P, N], U8, name="key_scales", align_bytes=64)
+        picked_scales = [sb.tile([P, HALF], U8, name="picked_scales%d" % h, align_bytes=64) for h in range(N // HALF)]
+        key_scales = [sb.tile([P, HALF], U8, name="key_scales%d" % h, align_bytes=64) for h in range(N // HALF)]
 
         nc.vector.memset(pool_scales[:].bitcast(I32), 0)
-        nc.vector.memset(key_scales[:].bitcast(I32), 0)
+        for plane in key_scales:
+            nc.vector.memset(plane[:].bitcast(I32), 0)
         nc.sync.dma_start(out=q_raw[:], in_=qT[0].rearrange("(p t) q -> p t q", t=PACK))
         nc.sync.dma_start(offsets[:], offs)
         nc.sync.dma_start(out=pool_scales[32:96:4, :].bitcast(I32), in_=k_scales[0].bitcast(I32))
@@ -59,12 +60,13 @@ def tile_attend_pagelse_kernel(tc, qT, k_words, k_scales, offs, out):
         nc.scalar.activation(out=q_bf[:], in_=q_raw[:].rearrange("p t q -> p q t"), func=ACT.Copy, scale=-2.0)
 
         cols = HALF // 16
-        nc.vector.tensor_copy(picked_scales[:], pool_scales[:].indirect(offsets[:]))
-        for quad in range(4):
-            nc.scalar.dma_start(
-                out=key_scales[32 * quad : 32 * quad + 4, :].bitcast(I32),
-                in_=picked_scales[32 + 16 * quad : 48 + 16 * quad : 4, :].bitcast(I32),
-            )
+        for h in range(N // HALF):
+            nc.vector.tensor_copy(picked_scales[h][:], pool_scales[:].indirect(offsets[:, h * cols : (h + 1) * cols]))
+            for quad in range(4):
+                nc.scalar.dma_start(
+                    out=key_scales[h][32 * quad : 32 * quad + 4, :].bitcast(I32),
+                    in_=picked_scales[h][32 + 16 * quad : 48 + 16 * quad : 4, :].bitcast(I32),
+                )
         nc.vector.quantize_mx(out=q_codes[:].bitcast(FP8X4), scales=q_scales[:], in_=q_bf[:].rearrange("p q t -> p (q t)"))
         for h in range(N // HALF):
             nc.vector.tensor_copy(key_words[h][:], pool_words[:].bitcast(U32).indirect(offsets[:, h * cols : (h + 1) * cols]))
@@ -80,7 +82,7 @@ def tile_attend_pagelse_kernel(tc, qT, k_words, k_scales, offs, out):
                 lhsT=q_codes[:].bitcast(FP8X4),
                 lhsT_scale=q_scales[:],
                 rhs=key_words[h][:, first : first + CHUNK].bitcast(FP8X4),
-                rhs_scale=key_scales[:, c * CHUNK : (c + 1) * CHUNK],
+                rhs_scale=key_scales[h][:, first : first + CHUNK],
                 start=True,
                 stop=True,
             )

@@ -21,7 +21,6 @@ HALF = 512
 CHUNK = 128
 CHUNK_PAGES = CHUNK // SEG
 WIDE = (5, 6, 7,)
-EARLY_LOADS = 2
 EARLY = 1024
 
 FLOPS = 2 * NQ * N * D
@@ -53,9 +52,9 @@ def tile_attend_pagelse_kernel(tc, qT, k_words, k_scales, offs, out):
         nc.sync.dma_start(offsets[:], offs)
         nc.sync.dma_start(out=pool_scales[32:96:4, :].bitcast(I32), in_=k_scales[0].bitcast(I32))
         words_hbm = k_words[0].rearrange("p n t -> p (n t)").bitcast(I32)
-        for r in range(EARLY_LOADS):
-            nc.sync.dma_start(out=pool_words[r:P:EARLY_LOADS, 0:EARLY], in_=words_hbm[r:P:EARLY_LOADS, 0:EARLY])
-        nc.sync.dma_start(out=pool_words[:, EARLY:T], in_=words_hbm[:, EARLY:T])
+        nc.sync.dma_start(out=pool_words[0:P:2, 0:EARLY], in_=words_hbm[0:P:2, 0:EARLY])
+        nc.sync.dma_start(out=pool_words[1:P:2, :], in_=words_hbm[1:P:2, :])
+        nc.sync.dma_start(out=pool_words[0:P:2, EARLY:T], in_=words_hbm[0:P:2, EARLY:T])
 
         nc.scalar.activation(out=q_bf[:], in_=q_raw[:].rearrange("p t q -> p q t"), func=ACT.Copy, scale=-2.0)
 

@@ -63,7 +63,7 @@ def tile_attend_pagelse_kernel(tc, qT, k_words, k_scales, offs, out):
             nc.vector.tensor_copy(picked_scales[h][:], pool_scales[:].indirect(offsets[:, h * cols : (h + 1) * cols]))
             for quad in range(4):
                 nc.scalar.dma_start(
-                    out=key_scales[h][32 * quad : 32 * quad + 4, :].bitcast(I32),
+                    out=key_scales[h][32 * quad + 4 * h : 32 * quad + 4 * h + 4, :].bitcast(I32),
                     in_=picked_scales[h][32 + 16 * quad : 48 + 16 * quad : 4, :].bitcast(I32),
                 )
         nc.vector.quantize_mx(out=q_codes[:].bitcast(FP8X4), scales=q_scales[:], in_=q_bf[:].rearrange("p q t -> p (q t)"))
@@ -81,7 +81,7 @@ def tile_attend_pagelse_kernel(tc, qT, k_words, k_scales, offs, out):
                 lhsT=q_codes[:].bitcast(FP8X4),
                 lhsT_scale=q_scales[:],
                 rhs=key_words[h][:, first : first + CHUNK].bitcast(FP8X4),
-                rhs_scale=key_scales[h][:, first : first + CHUNK],
+                rhs_scale=key_scales[h][4 * h :, first : first + CHUNK],
                 start=True,
                 stop=True,
             )

@@ -17,11 +17,13 @@ P = 128
 PACK = 4
 D, T, N, NQ, SEG = 512, 4096, 1024, 128, 32
 PAGES = N // SEG
-HALF = 512
-CHUNK = 128
-CHUNK_PAGES = CHUNK // SEG
-WIDE = (5, 6, 7,)
-EARLY = 1024
+PIECE = 256
+RUN = 128
+RUNS = N // RUN
+RUN_PAGES = RUN // SEG
+SHIFTED_RUNS = 3
+EARLY = 512
+VECTOR_ZEROES = 448
 
 FLOPS = 2 * NQ * N * D
 BYTES = D * NQ * 4 + T * P * 4 + 16 * T + P * 64 * 2 + NQ * PAGES * 4
@@ -41,104 +43,82 @@ def tile_attend_pagelse_kernel(tc, qT, k_words, k_scales, offs, out):
         q_bf = sb.tile([P, NQ, PACK], BF16, name="q_bf", align_bytes=64)
         q_codes = sb.tile([P, NQ], U32, name="q_codes", align_bytes=64)
         q_scales = sb.tile([P, NQ], U8, name="q_scales", align_bytes=64)
-        key_words = [sb.tile([P, HALF], U32, name="key_words%d" % h, align_bytes=64) for h in range(N // HALF)]
-        picked_scales = [sb.tile([P, HALF], U8, name="picked_scales%d" % h, align_bytes=64) for h in range(N // HALF)]
-        key_scales = [sb.tile([P, HALF], U8, name="key_scales%d" % h, align_bytes=64) for h in range(N // HALF)]
+        key_words = [sb.tile([P, PIECE], U32, name="key_words%d" % g, align_bytes=64) for g in range(N // PIECE)]
+        picked_scales = sb.tile([P, N], U8, name="picked_scales", align_bytes=64)
+        key_scales = sb.tile([P, N], U8, name="key_scales", align_bytes=64)
 
-        nc.vector.memset(pool_scales[:].bitcast(I32), 0)
-        for plane in key_scales:
-            nc.vector.memset(plane[:].bitcast(I32), 0)
+        pool_scale_words = pool_scales[:].bitcast(I32)
+        nc.vector.memset(pool_scale_words[:, 0 : VECTOR_ZEROES - 1], 0)
+        nc.vector.memset(pool_scale_words[:, VECTOR_ZEROES - 1 : VECTOR_ZEROES], 0)
+        nc.gpsimd.memset(pool_scale_words[:, VECTOR_ZEROES : T // 4], 0)
+        nc.vector.memset(key_scales[:].bitcast(I32), 0)
+
+        words_hbm = k_words[0].rearrange("p n t -> p (n t)").bitcast(I32)
         nc.sync.dma_start(out=q_raw[:], in_=qT[0].rearrange("(p t) q -> p t q", t=PACK))
         nc.sync.dma_start(offsets[:], offs)
-        nc.sync.dma_start(out=pool_scales[32:96:4, :].bitcast(I32), in_=k_scales[0].bitcast(I32))
-        words_hbm = k_words[0].rearrange("p n t -> p (n t)").bitcast(I32)
         nc.sync.dma_start(out=pool_words[0:P:2, 0:EARLY], in_=words_hbm[0:P:2, 0:EARLY])
+        nc.sync.dma_start(out=pool_scale_words[32:96:4, :], in_=k_scales[0].bitcast(I32))
         nc.sync.dma_start(out=pool_words[1:P:2, :], in_=words_hbm[1:P:2, :])
         nc.sync.dma_start(out=pool_words[0:P:2, EARLY:T], in_=words_hbm[0:P:2, EARLY:T])
 
         nc.scalar.activation(out=q_bf[:], in_=q_raw[:].rearrange("p t q -> p q t"), func=ACT.Copy, scale=-2.0)
 
-        cols = HALF // 16
-        for h in range(N // HALF):
-            nc.vector.tensor_copy(picked_scales[h][:], pool_scales[:].indirect(offsets[:, h * cols : (h + 1) * cols]))
-            for quad in range(4):
-                nc.scalar.dma_start(
-                    out=key_scales[h][32 * quad + 4 * h : 32 * quad + 4 * h + 4, :].bitcast(I32),
-                    in_=picked_scales[h][32 + 16 * quad : 48 + 16 * quad : 4, :].bitcast(I32),
-                )
+        nc.vector.tensor_copy(picked_scales[:], pool_scales[:].indirect(offsets[:]))
+        for quad in range(4):
+            nc.scalar.dma_start(
+                out=key_scales[32 * quad : 32 * quad + 4, :].bitcast(I32),
+                in_=picked_scales[32 + 16 * quad : 48 + 16 * quad : 4, :].bitcast(I32),
+            )
         nc.vector.quantize_mx(out=q_codes[:].bitcast(FP8X4), scales=q_scales[:], in_=q_bf[:].rearrange("p q t -> p (q t)"))
-        for h in range(N // HALF):
-            nc.vector.tensor_copy(key_words[h][:], pool_words[:].bitcast(U32).indirect(offsets[:, h * cols : (h + 1) * cols]))
+        cols = PIECE // 16
+        for g in range(N // PIECE):
+            nc.vector.tensor_copy(key_words[g][:], pool_words[:].bitcast(U32).indirect(offsets[:, g * cols : (g + 1) * cols]))
 
         least = sb.tile([P, PAGES], F32, name="least")
         sums = sb.tile([P, PAGES], F32, name="sums")
         scores = []
-        for c in range(N // CHUNK):
-            bank = ps.tile([NQ, CHUNK], F32, name="bank%d" % c)
-            h, first = divmod(c * CHUNK, HALF)
+        for c in range(RUNS):
+            bank = ps.tile([NQ, RUN], F32, name="bank%d" % c)
+            g, first = divmod(c * RUN, PIECE)
             nc.tensor.matmul_mx(
                 out=bank[:],
                 lhsT=q_codes[:].bitcast(FP8X4),
                 lhsT_scale=q_scales[:],
-                rhs=key_words[h][:, first : first + CHUNK].bitcast(FP8X4),
-                rhs_scale=key_scales[h][4 * h :, first : first + CHUNK],
+                rhs=key_words[g][:, first : first + RUN].bitcast(FP8X4),
+                rhs_scale=key_scales[:, c * RUN : (c + 1) * RUN],
                 start=True,
                 stop=True,
             )
             scores.append(bank[:].rearrange("q (j i) -> q j i", i=SEG))
 
         def pages_of(c):
-            return slice(c * CHUNK_PAGES, (c + 1) * CHUNK_PAGES)
+            return slice(c * RUN_PAGES, (c + 1) * RUN_PAGES)
 
-        all_terms = sb.tile([P, PAGES, SEG], F32, name="all_terms")
-        terms = [all_terms[:, pages_of(c), :] for c in range(N // CHUNK)]
-        shifted = {c: sb.tile([P, CHUNK_PAGES, SEG], F32, name="shifted%d" % c) for c in WIDE}
+        terms = sb.tile([P, PAGES, SEG], F32, name="terms")
+        by_page_runs = RUNS - SHIFTED_RUNS
 
-        def find_least(c):
+        for c in range(RUNS):
             nc.vector.tensor_reduce(out=least[:, pages_of(c)], in_=scores[c], axis=AXIS_X, op=ALU.min)
-
-        def by_page(c):
-            for j in range(CHUNK_PAGES):
-                page = c * CHUNK_PAGES + j
-                nc.scalar.activation(
-                    out=terms[c][:, j, :],
-                    in_=scores[c][:, j, :],
-                    func=ACT.Exp,
-                    bias=least[:, page : page + 1],
-                    scale=-1.0,
-                )
-
-        def shift(c):
+            if c < by_page_runs:
+                for j in range(RUN_PAGES):
+                    page = c * RUN_PAGES + j
+                    nc.scalar.activation(
+                        out=terms[:, page, :],
+                        in_=scores[c][:, j, :],
+                        func=ACT.Exp,
+                        bias=least[:, page : page + 1],
+                        scale=-1.0,
+                    )
+        for c in range(by_page_runs, RUNS):
+            shifted = sb.tile([P, RUN_PAGES, SEG], F32, name="shifted%d" % c)
             nc.vector.tensor_tensor(
-                out=shifted[c][:],
+                out=shifted[:],
                 in0=scores[c],
-                in1=least[:, pages_of(c)].unsqueeze(2).to_broadcast([P, CHUNK_PAGES, SEG]),
+                in1=least[:, pages_of(c)].unsqueeze(2).to_broadcast([P, RUN_PAGES, SEG]),
                 op=ALU.subtract,
             )
-
-        def wide_exp(c):
-            nc.scalar.activation(out=terms[c], in_=shifted[c][:], func=ACT.Exp, scale=-1.0)
-
-        find_least(0)
-        by_page(0)
-        find_least(1)
-        by_page(1)
-        find_least(2)
-        by_page(2)
-        find_least(3)
-        by_page(3)
-        find_least(4)
-        by_page(4)
-        find_least(5)
-        find_least(6)
-        shift(5)
-        wide_exp(5)
-        find_least(7)
-        shift(6)
-        wide_exp(6)
-        shift(7)
-        wide_exp(7)
-        nc.vector.tensor_reduce(out=sums[:], in_=all_terms[:], axis=AXIS_X, op=ALU.add)
+            nc.scalar.activation(out=terms[:, pages_of(c), :], in_=shifted[:], func=ACT.Exp, scale=-1.0)
+        nc.vector.tensor_reduce(out=sums[:], in_=terms[:], axis=AXIS_X, op=ALU.add)
 
         logs = sb.tile([P, PAGES], F32, name="logs")
         result = sb.tile([P, PAGES], F32, name="result")

@@ -22,8 +22,8 @@ RUN = 128
 RUNS = N // RUN
 RUN_PAGES = RUN // SEG
 SHIFTED_RUNS = 3
-EARLY = 512
-VECTOR_ZEROES = 448
+EARLY = 1024
+HALF = N // 2
 
 FLOPS = 2 * NQ * N * D
 BYTES = D * NQ * 4 + T * P * 4 + 16 * T + P * 64 * 2 + NQ * PAGES * 4
@@ -34,24 +34,24 @@ def tile_attend_pagelse_kernel(tc, qT, k_words, k_scales, offs, out):
 
     with ExitStack() as ctx:
         sb = ctx.enter_context(tc.tile_pool(name="sb", bufs=1))
+        shared = ctx.enter_context(tc.tile_pool(name="shared", bufs=1))
         ps = ctx.enter_context(tc.psum_pool(name="ps", bufs=1))
 
         offsets = sb.tile([P, N // 16], U16, name="offsets")
         pool_words = sb.tile([P, T], I32, name="pool_words", align_bytes=64)
-        pool_scales = sb.tile([P, T], U8, name="pool_scales", align_bytes=64)
+        pool_scales = shared.tile([P, T], U8, name="pool_scales", align_bytes=64, offset=0)
         q_raw = sb.tile([P, PACK, NQ], F32, name="q_raw", align_bytes=64)
         q_bf = sb.tile([P, NQ, PACK], BF16, name="q_bf", align_bytes=64)
-        q_codes = sb.tile([P, NQ], U32, name="q_codes", align_bytes=64)
-        q_scales = sb.tile([P, NQ], U8, name="q_scales", align_bytes=64)
+        q_codes = shared.tile([P, NQ], U32, name="q_codes", align_bytes=64, offset=0)
+        q_scales = shared.tile([P, NQ], U8, name="q_scales", align_bytes=64, offset=4 * NQ)
         key_words = [sb.tile([P, PIECE], U32, name="key_words%d" % g, align_bytes=64) for g in range(N // PIECE)]
-        picked_scales = sb.tile([P, N], U8, name="picked_scales", align_bytes=64)
-        key_scales = sb.tile([P, N], U8, name="key_scales", align_bytes=64)
+        picked_scales = [sb.tile([P, HALF], U8, name="picked_scales%d" % h, align_bytes=64) for h in range(2)]
+        key_scales = [sb.tile([P, HALF], U8, name="key_scales%d" % h, align_bytes=64) for h in range(2)]
 
         pool_scale_words = pool_scales[:].bitcast(I32)
-        nc.vector.memset(pool_scale_words[:, 0 : VECTOR_ZEROES - 1], 0)
-        nc.vector.memset(pool_scale_words[:, VECTOR_ZEROES - 1 : VECTOR_ZEROES], 0)
-        nc.gpsimd.memset(pool_scale_words[:, VECTOR_ZEROES : T // 4], 0)
-        nc.vector.memset(key_scales[:].bitcast(I32), 0)
+        nc.vector.memset(pool_scale_words, 0)
+        for plane in key_scales:
+            nc.vector.memset(plane[:].bitcast(I32), 0)
 
         words_hbm = k_words[0].rearrange("p n t -> p (n t)").bitcast(I32)
         nc.sync.dma_start(out=q_raw[:], in_=qT[0].rearrange("(p t) q -> p t q", t=PACK))
@@ -63,12 +63,16 @@ def tile_attend_pagelse_kernel(tc, qT, k_words, k_scales, offs, out):
 
         nc.scalar.activation(out=q_bf[:], in_=q_raw[:].rearrange("p t q -> p q t"), func=ACT.Copy, scale=-2.0)
 
-        nc.vector.tensor_copy(picked_scales[:], pool_scales[:].indirect(offsets[:]))
-        for quad in range(4):
-            nc.scalar.dma_start(
-                out=key_scales[32 * quad : 32 * quad + 4, :].bitcast(I32),
-                in_=picked_scales[32 + 16 * quad : 48 + 16 * quad : 4, :].bitcast(I32),
+        half_cols = HALF // 16
+        for h in range(2):
+            nc.vector.tensor_copy(
+                picked_scales[h][:], pool_scales[:].indirect(offsets[:, h * half_cols : (h + 1) * half_cols])
             )
+            for quad in range(4):
+                nc.scalar.dma_start(
+                    out=key_scales[h][32 * quad + 4 * h : 32 * quad + 4 * h + 4, :].bitcast(I32),
+                    in_=picked_scales[h][32 + 16 * quad : 48 + 16 * quad : 4, :].bitcast(I32),
+                )
         nc.vector.quantize_mx(out=q_codes[:].bitcast(FP8X4), scales=q_scales[:], in_=q_bf[:].rearrange("p q t -> p (q t)"))
         cols = PIECE // 16
         for g in range(N // PIECE):
@@ -80,12 +84,13 @@ def tile_attend_pagelse_kernel(tc, qT, k_words, k_scales, offs, out):
         for c in range(RUNS):
             bank = ps.tile([NQ, RUN], F32, name="bank%d" % c)
             g, first = divmod(c * RUN, PIECE)
+            h, plane_first = divmod(c * RUN, HALF)
             nc.tensor.matmul_mx(
                 out=bank[:],
                 lhsT=q_codes[:].bitcast(FP8X4),
                 lhsT_scale=q_scales[:],
                 rhs=key_words[g][:, first : first + RUN].bitcast(FP8X4),
-                rhs_scale=key_scales[:, c * RUN : (c + 1) * RUN],
+                rhs_scale=key_scales[h][4 * h :, plane_first : plane_first + RUN],
                 start=True,
                 stop=True,
             )

from contextlib import ExitStack

import concourse.mybir as mybir

F32 = mybir.dt.float32
BF16 = mybir.dt.bfloat16
I32 = mybir.dt.int32
U32 = mybir.dt.uint32
U16 = mybir.dt.uint16
U8 = mybir.dt.uint8
FP8X4 = mybir.dt.float8_e4m3fn_x4
ALU = mybir.AluOpType
ACT = mybir.ActivationFunctionType
AXIS_X = mybir.AxisListType.X

P = 128
PACK = 4
D, T, N, NQ, SEG = 512, 4096, 1024, 128, 32
PAGES = N // SEG
PIECE = 256
RUN = 128
RUNS = N // RUN
RUN_PAGES = RUN // SEG
SHIFTED_RUNS = 3
EARLY = 1024
HALF = N // 2

FLOPS = 2 * NQ * N * D
BYTES = D * NQ * 4 + T * P * 4 + 16 * T + P * 64 * 2 + NQ * PAGES * 4


def tile_attend_pagelse_kernel(tc, qT, k_words, k_scales, offs, out):
    nc = tc.nc

    with ExitStack() as ctx:
        sb = ctx.enter_context(tc.tile_pool(name="sb", bufs=1))
        shared = ctx.enter_context(tc.tile_pool(name="shared", bufs=1))
        ps = ctx.enter_context(tc.psum_pool(name="ps", bufs=1))

        offsets = sb.tile([P, N // 16], U16, name="offsets")
        pool_words = sb.tile([P, T], I32, name="pool_words", align_bytes=64)
        pool_scales = shared.tile([P, T], U8, name="pool_scales", align_bytes=64, offset=0)
        q_raw = sb.tile([P, PACK, NQ], F32, name="q_raw", align_bytes=64)
        q_bf = sb.tile([P, NQ, PACK], BF16, name="q_bf", align_bytes=64)
        q_codes = shared.tile([P, NQ], U32, name="q_codes", align_bytes=64, offset=0)
        q_scales = shared.tile([P, NQ], U8, name="q_scales", align_bytes=64, offset=4 * NQ)
        key_words = [sb.tile([P, PIECE], U32, name="key_words%d" % g, align_bytes=64) for g in range(N // PIECE)]
        picked_scales = [sb.tile([P, HALF], U8, name="picked_scales%d" % h, align_bytes=64) for h in range(2)]
        key_scales = [sb.tile([P, HALF], U8, name="key_scales%d" % h, align_bytes=64) for h in range(2)]

        pool_scale_words = pool_scales[:].bitcast(I32)
        nc.vector.memset(pool_scale_words, 0)
        for plane in key_scales:
            nc.vector.memset(plane[:].bitcast(I32), 0)

        words_hbm = k_words[0].rearrange("p n t -> p (n t)").bitcast(I32)
        nc.sync.dma_start(out=q_raw[:], in_=qT[0].rearrange("(p t) q -> p t q", t=PACK))
        nc.sync.dma_start(offsets[:], offs)
        nc.sync.dma_start(out=pool_words[0:P:2, 0:EARLY], in_=words_hbm[0:P:2, 0:EARLY])
        nc.sync.dma_start(out=pool_scale_words[32:96:4, :], in_=k_scales[0].bitcast(I32))
        nc.sync.dma_start(out=pool_words[1:P:2, :], in_=words_hbm[1:P:2, :])
        nc.sync.dma_start(out=pool_words[0:P:2, EARLY:T], in_=words_hbm[0:P:2, EARLY:T])

        nc.scalar.activation(out=q_bf[:], in_=q_raw[:].rearrange("p t q -> p q t"), func=ACT.Copy, scale=-2.0)

        half_cols = HALF // 16
        for h in range(2):
            nc.vector.tensor_copy(
                picked_scales[h][:], pool_scales[:].indirect(offsets[:, h * half_cols : (h + 1) * half_cols])
            )
            for quad in range(4):
                nc.scalar.dma_start(
                    out=key_scales[h][32 * quad + 4 * h : 32 * quad + 4 * h + 4, :].bitcast(I32),
                    in_=picked_scales[h][32 + 16 * quad : 48 + 16 * quad : 4, :].bitcast(I32),
                )
        nc.vector.quantize_mx(out=q_codes[:].bitcast(FP8X4), scales=q_scales[:], in_=q_bf[:].rearrange("p q t -> p (q t)"))
        cols = PIECE // 16
        for g in range(N // PIECE):
            nc.vector.tensor_copy(key_words[g][:], pool_words[:].bitcast(U32).indirect(offsets[:, g * cols : (g + 1) * cols]))

        least = sb.tile([P, PAGES], F32, name="least")
        sums = sb.tile([P, PAGES], F32, name="sums")
        scores = []
        for c in range(RUNS):
            bank = ps.tile([NQ, RUN], F32, name="bank%d" % c)
            g, first = divmod(c * RUN, PIECE)
            h, plane_first = divmod(c * RUN, HALF)
            nc.tensor.matmul_mx(
                out=bank[:],
                lhsT=q_codes[:].bitcast(FP8X4),
                lhsT_scale=q_scales[:],
                rhs=key_words[g][:, first : first + RUN].bitcast(FP8X4),
                rhs_scale=key_scales[h][4 * h :, plane_first : plane_first + RUN],
                start=True,
                stop=True,
            )
            scores.append(bank[:].rearrange("q (j i) -> q j i", i=SEG))

        def pages_of(c):
            return slice(c * RUN_PAGES, (c + 1) * RUN_PAGES)

        terms = sb.tile([P, PAGES, SEG], F32, name="terms")
        by_page_runs = RUNS - SHIFTED_RUNS

        for c in range(RUNS):
            nc.vector.tensor_reduce(out=least[:, pages_of(c)], in_=scores[c], axis=AXIS_X, op=ALU.min)
            if c < by_page_runs:
                for j in range(RUN_PAGES):
                    page = c * RUN_PAGES + j
                    nc.scalar.activation(
                        out=terms[:, page, :],
                        in_=scores[c][:, j, :],
                        func=ACT.Exp,
                        bias=least[:, page : page + 1],
                        scale=-1.0,
                    )
        for c in range(by_page_runs, RUNS):
            shifted = sb.tile([P, RUN_PAGES, SEG], F32, name="shifted%d" % c)
            nc.vector.tensor_tensor(
                out=shifted[:],
                in0=scores[c],
                in1=least[:, pages_of(c)].unsqueeze(2).to_broadcast([P, RUN_PAGES, SEG]),
                op=ALU.subtract,
            )
            nc.scalar.activation(out=terms[:, pages_of(c), :], in_=shifted[:], func=ACT.Exp, scale=-1.0)
        nc.vector.tensor_reduce(out=sums[:], in_=terms[:], axis=AXIS_X, op=ALU.add)

        logs = sb.tile([P, PAGES], F32, name="logs")
        result = sb.tile([P, PAGES], F32, name="result")
        nc.scalar.activation(out=logs[:], in_=sums[:], func=ACT.Ln)
        nc.vector.tensor_tensor(out=result[:], in0=logs[:], in1=least[:], op=ALU.subtract)
        nc.sync.dma_start(out=out[0], in_=result[:])
